import numpy as np
import ml_dtypes


def mxq(x, axis, fmt="e4m3"):
    dtype, down = {"e4m3": (ml_dtypes.float8_e4m3fn, 7), "e5m2": (ml_dtypes.float8_e5m2, 14)}[fmt]
    v = np.moveaxis(np.asarray(x, np.float32).astype(ml_dtypes.bfloat16).astype(np.float64), axis, -1)
    blocks = v.reshape(v.shape[:-1] + (-1, 32))
    amax = np.abs(blocks).max(-1, keepdims=True)
    byte = np.maximum(np.where(amax > 0, np.frexp(amax)[1] - 1 + 127, 0) - down, 1)
    scale = np.exp2(byte - 127.0)
    codes = (blocks / scale).astype(np.float32).astype(dtype).astype(np.float64)
    return np.moveaxis((codes * scale).reshape(v.shape), -1, axis)


WIDE = False


def mx_kscale(k):
    if not WIDE:
        return np.ones(k)
    levels = np.array([10, -10, 5, -5, 0])
    if k % 512:
        return np.exp2(np.random.permutation(np.resize(levels, k // 32))).repeat(32)
    a = np.empty((k // 512, 16))
    for p in range(k // 512):
        a[p, :8] = np.random.permutation(np.resize(levels, 8))
        for g in range(8):
            far = levels[np.abs(levels - a[p, g]) >= 10]
            a[p, g + 8] = far[np.random.randint(len(far))]
    return np.exp2(a.ravel()).repeat(32)


def f64(x):
    return np.asarray(x).astype(np.float64)


def striped(idx):
    return np.tile(idx.reshape(-1, 16).T, (8, 1)).astype(np.uint16)


def unstriped(offs):
    return offs[:16].T.reshape(-1).astype(np.int64)


def pack_weight(w):
    k, n = w.shape
    w = f64(np.asarray(w, np.float32).astype(ml_dtypes.bfloat16)).reshape(k // 32, 32, n)
    amax = np.abs(w).max(1)
    byte = np.clip(np.where(amax > 0, np.frexp(amax)[1] - 1 + 127 - 7, 1), 1, 254)
    scaled = (w * np.exp2(127.0 - byte)[:, None, :]).reshape(k, n).astype(np.float32)
    words = np.ascontiguousarray(scaled.reshape(k // 512, 128, 4, n).transpose(0, 1, 3, 2)).astype(ml_dtypes.float8_e4m3fn).view(np.uint8)
    return words, np.ascontiguousarray(byte.astype(np.uint8).reshape(k // 512, 16, n))


def unpack_weight(words, scales):
    g, p, n, _ = words.shape
    vals = np.ascontiguousarray(words).view(ml_dtypes.float8_e4m3fn).astype(np.float64) * np.repeat(np.exp2(scales.astype(np.float64) - 127.0), 8, axis=1)[..., None]
    return vals.transpose(0, 1, 3, 2).reshape(g * 512, n)


K, T, S, D, N, H, V, U = 1024, 2048, 1024, 4, 256, 512, 256, 512


def setup_inputs():
    n = np.random.standard_normal
    s = mx_kscale(K)[:, None]
    u = mx_kscale(H)
    packed_xT = pack_weight(n((K, T)) * s)
    return {
        "x_words": packed_xT[0],
        "x_scales": packed_xT[1],
        "w1": (n((K, H)) / np.sqrt(K) / s).astype(np.float32),
        "w2": (n((K, H)) / np.sqrt(K) / s).astype(np.float32),
        "px": (1.5 * n((H, U))).astype(np.float32),
        "unit": (np.random.uniform(0.6, 1.4, (H, 1)) * u[:, None]).astype(np.float32),
        "w3": (n((H, N)) / np.sqrt(H) / u[:, None]).astype(np.float32),
        "offs": striped(np.random.permutation(T)[:S]),
        "nd": striped(np.random.permutation(np.concatenate([np.arange(V), np.random.randint(0, V, U - V)]))),
    }


def reference(x_words, x_scales, w1, w2, px, unit, w3, offs, nd):
    xq = unpack_weight(x_words, x_scales)[:, unstriped(offs)]
    ms = mxq(f64(w1), 0, "e4m3").T @ xq
    mass = np.log(np.exp(ms) + 1.0) + 0.2
    mtot = mass.reshape(len(mass), -1, D).sum(axis=2)
    mn = mtot[:, unstriped(nd)]
    cx = mxq(f64(w2), 0, "e4m3").T @ xq
    mx_ = mass * cx
    com = (mx_.reshape(len(mx_), -1, D).sum(axis=2)) / mtot
    cn = com[:, unstriped(nd)]
    sep = f64(px) - cn
    r2 = (sep) ** 2 + 0.6
    mono = (mn * sep) / r2
    mq = mass * ((cx - np.repeat(com, D, axis=1)) ** 2)
    quad = mq.reshape(len(mq), -1, D).sum(axis=2)
    qn = quad[:, unstriped(nd)]
    qua = (qn * sep) / ((r2) ** 2)
    hid = f64(unit) * (mono + 1.5 * qua)
    return mxq(f64(w3), 0, "e4m3").T @ mxq(hid, 0, "e4m3")

@@ -1,0 +1,329 @@
+from contextlib import ExitStack
+
+import concourse.mybir as mybir
+from concourse.masks import make_identity
+
+K, T, S, D, N, H, V, U = 1024, 2048, 1024, 4, 256, 512, 256, 512
+FLOPS = 2 * (2 * K * H * S + H * N * U)
+
+F32 = mybir.dt.float32
+BF16 = mybir.dt.bfloat16
+I32 = mybir.dt.int32
+U32 = mybir.dt.uint32
+U16 = mybir.dt.uint16
+U8 = mybir.dt.uint8
+FP8X4 = mybir.dt.float8_e4m3fn_x4
+ALU = mybir.AluOpType
+ACT = mybir.ActivationFunctionType
+
+P = 128
+PACK = 4
+PASSES = K // (P * PACK)
+VBLOCKS = V // P
+WINDOW = U + 16
+HALF = U // 2
+LN_FLOOR = 2.0 ** -60
+
+
+def tile_picked_ynbodyt_acc_p_kernel(
+    tc, x_words, x_scales, w1, w2, px, unit, w3, offs, nd, out
+):
+    nc = tc.nc
+    with ExitStack() as ctx:
+        keep = ctx.enter_context(tc.tile_pool(name="keep", bufs=1))
+        ring = ctx.enter_context(tc.tile_pool(name="ring", bufs=2))
+        psum = ctx.enter_context(tc.psum_pool(name="psum", bufs=1))
+
+        def held(shape, dtype, name):
+            return keep.tile(shape, dtype, name=name, align_bytes=64)
+
+        def bank(name, number):
+            return psum.tile([P, 512], F32, name=name, tag="bank%d" % number)
+
+        offs_sb = keep.tile([P, S // 16], U16, name="offs_sb")
+        nc.sync.dma_start(offs_sb[:], offs)
+        nd_sb = keep.tile([P, U // 16], U16, name="nd_sb")
+        nc.sync.dma_start(nd_sb[:], nd)
+        unit_sb = held([P, PACK], F32, "unit_sb")
+        nc.sync.dma_start(unit_sb[:], unit.rearrange("(p t) o -> p (t o)", t=PACK))
+
+        xs_table = held([P, T], U8, "xs_table")
+        nc.gpsimd.memset(xs_table[:].bitcast(I32), 0)
+        for q in range(4):
+            nc.scalar.dma_start(
+                xs_table[32 * q : 32 * q + 4 * PASSES, :].bitcast(I32),
+                x_scales[:, 4 * q : 4 * q + 4, :].bitcast(I32),
+            )
+
+        def load_words(g):
+            table = held([P, T], U32, "xw_table%d" % g)
+            nc.sync.dma_start(table[:].bitcast(I32), x_words[g].rearrange("p n j -> p (n j)").bitcast(I32))
+            return table
+
+        def load_rows(w, g, name):
+            raw = held([P, PACK, w.shape[1]], F32, name)
+            nc.sync.dma_start(raw[:], w[512 * g : 512 * (g + 1), :].rearrange("(p j) c -> p j c", j=PACK))
+            return raw
+
+        xw_table = []
+        w1_raw = []
+        for g in range(PASSES):
+            xw_table.append(load_words(g))
+            w1_raw.append(load_rows(w1, g, "w1_raw%d" % g))
+        w2_raw = [load_rows(w2, g, "w2_raw%d" % g) for g in range(PASSES)]
+        px_sb = load_rows(px, 0, "px_sb")
+        w3_raw = load_rows(w3, 0, "w3_raw")
+
+        ident = held([P, P], F32, "ident")
+        make_identity(nc, ident[:])
+
+        tables = {}
+        for t in range(PACK):
+            for name in ("ncom", "mtot", "quad"):
+                table = held([P, WINDOW], F32, "%s%d" % (name, t))
+                nc.vector.memset(table[:, V:WINDOW], 0.0)
+                tables[name, t] = table
+
+        def scaled_unit(factor, name):
+            scaled = held([P, PACK], F32, name)
+            nc.gpsimd.tensor_scalar(scaled[:], unit_sb[:], factor, 0.0, ALU.mult, ALU.add)
+            return scaled
+
+        unit_neg = scaled_unit(-1.0, "unit_neg")
+        unit_base = scaled_unit(D * 0.2, "unit_base")
+        unit_quad = scaled_unit(-1.5, "unit_quad")
+
+        def pick(table, dtype, view, vb, name, tag=""):
+            picked = keep.tile([P, D * P], dtype, name=name + "_picked", tag=tag, align_bytes=64)
+            nc.vector.tensor_copy(picked[:], table[:].indirect(offs_sb[:, 32 * vb : 32 * (vb + 1)]))
+            dealt = held([P, D, P], dtype, name + "_dealt")
+            nc.vector.tensor_copy(
+                dealt[:].bitcast(view).rearrange("p d v -> p v d"),
+                picked[:].bitcast(view).rearrange("p (v d) -> p v d", d=D),
+            )
+            return dealt
+
+        def round_weights(copy, raw, name):
+            grouped = keep.tile([P, PACK, P, PACK], BF16, name=name, tag=name, align_bytes=64)
+            copy(
+                grouped[:].rearrange("p t m j -> p m j t"),
+                raw[:].rearrange("p j (m t) -> p m j t", t=PACK),
+            )
+            return grouped
+
+        def quantize(grouped, words, pieces, name):
+            codes = held([P, words], U32, name + "_codes")
+            scales = held([P, words], U8, name + "_scales")
+            step = words // pieces
+            for a in range(0, words, step):
+                nc.vector.quantize_mx(
+                    out=codes[:, a : a + step].bitcast(FP8X4),
+                    scales=scales[:, a : a + step],
+                    in_=grouped[:, PACK * a : PACK * (a + step)],
+                )
+            return codes, scales
+
+        def flat(grouped):
+            return grouped[:].rearrange("p t m j -> p (t m j)")
+
+        xs = {}
+        xw = {}
+        for vb in range(VBLOCKS):
+            xs[vb] = pick(xs_table, U8, U8, vb, "xs%d" % vb)
+        for vb in range(VBLOCKS):
+            xw[0, vb] = pick(xw_table[0], U32, I32, vb, "xw0%d" % vb)
+        w1_q = [quantize(flat(round_weights(nc.scalar.copy, w1_raw[0], "w1_grouped0")), H, 1, "w1_0")]
+        xw[1, 0] = pick(xw_table[1], U32, I32, 0, "xw10")
+        w1_q.append(quantize(flat(round_weights(nc.vector.tensor_copy, w1_raw[1], "w1_grouped1")), H, 1, "w1_1"))
+        xw[1, 1] = pick(xw_table[1], U32, I32, 1, "xw11", "w1_grouped1")
+
+        def product_pass(acc, w_q, g, t, vb):
+            codes, scales = w_q[g]
+            for d in range(D):
+                nc.tensor.matmul_mx(
+                    out=acc[:, P * d : P * (d + 1)],
+                    lhsT=xw[g, vb][:, d, :].bitcast(FP8X4),
+                    lhsT_scale=xs[vb][4 * g : P, d, :],
+                    rhs=codes[:, P * t : P * (t + 1)].bitcast(FP8X4),
+                    rhs_scale=scales[:, P * t : P * (t + 1)],
+                    start=(g == 0 and d == 0),
+                    stop=(g == PASSES - 1 and d == D - 1),
+                )
+
+        def product(w_q, t, vb, name, number):
+            acc = bank(name, number)
+            for g in range(PASSES):
+                product_pass(acc, w_q, g, t, vb)
+            return acc
+
+        ms = {}
+        nmass = {}
+        for t in range(PACK):
+            nmass[t] = held([P, VBLOCKS, D * P], F32, "nmass%d" % t)
+        for vb in range(VBLOCKS):
+            for t in range(PACK):
+                ms[t, vb] = bank("ms%d%d" % (t, vb), 2 * t + vb)
+                product_pass(ms[t, vb], w1_q, 0, t, vb)
+        for vb in range(VBLOCKS):
+            for t in (range(PACK) if vb == 0 else reversed(range(PACK))):
+                product_pass(ms[t, vb], w1_q, 1, t, vb)
+                nc.scalar.activation(nmass[t][:, vb, :], ms[t, vb][:], ACT.Sigmoid, scale=-1.0)
+
+        w2_q = []
+        for g in range(PASSES):
+            grouped = round_weights(nc.vector.tensor_copy, w2_raw[g], "w2_grouped%d" % g)
+            w2_q.append(quantize(flat(grouped), H, 1, "w2_%d" % g))
+
+        for t in range(PACK):
+            nc.scalar.activation(nmass[t][:], nmass[t][:], ACT.Ln, bias=LN_FLOOR)
+
+        w3_grouped = held([P, N, PACK], BF16, "w3_grouped")
+        nc.scalar.copy(
+            w3_grouped[:].rearrange("p (c i) j -> p c j i", i=4),
+            w3_raw[:].rearrange("p j (c i) -> p c j i", i=4),
+        )
+
+        def softplus(t):
+            for vb in range(VBLOCKS):
+                nc.vector.scalar_tensor_tensor(
+                    nmass[t][:, vb, :], ms[t, vb][:], -1.0, nmass[t][:, vb, :], ALU.mult, ALU.min
+                )
+
+        def group_sum(acc, column, values):
+            for d in range(D):
+                nc.tensor.matmul(
+                    acc[:, column : column + P],
+                    values[:, P * d : P * (d + 1)],
+                    ident[:],
+                    start=(d == 0),
+                    stop=(d == D - 1),
+                    is_transpose=True,
+                )
+
+        sums = {}
+
+        def moments(t):
+            cx = [product(w2_q, t, vb, "cx%d%d" % (t, vb), 4 * (t % 2) + vb) for vb in range(VBLOCKS)]
+            zeroth = bank("zeroth%d" % t, 4 * (t % 2) + 2)
+            for vb in range(VBLOCKS):
+                group_sum(zeroth, P * vb, nmass[t][:, vb, :])
+            higher = bank("higher%d" % t, 4 * (t % 2) + 3)
+            first = []
+            for vb in range(VBLOCKS):
+                value = ring.tile([P, D * P], F32, name="first%d%d" % (t, vb), tag="first", bufs=3)
+                nc.vector.scalar_tensor_tensor(
+                    value[:], nmass[t][:, vb, :], 0.2, cx[vb][:], ALU.subtract, ALU.mult
+                )
+                group_sum(higher, P * vb, value[:])
+                first.append(value)
+            for vb in range(VBLOCKS):
+                value = ring.tile([P, D * P], F32, name="second%d%d" % (t, vb), tag="second", bufs=3)
+                nc.vector.tensor_tensor(value[:], first[vb][:], cx[vb][:], ALU.mult)
+                group_sum(higher, V + P * vb, value[:])
+            sums[t] = (zeroth, higher)
+
+        def nodes(t):
+            zeroth, higher = sums[t]
+            inv = ring.tile([P, V], F32, name="inv%d" % t, tag="inv")
+            nc.scalar.activation(inv[:], zeroth[:, 0:V], ACT.Abs_reciprocal_sqrt, bias=D * 0.2, scale=-1.0)
+            nc.scalar.activation(inv[:], inv[:], ACT.Square)
+            nc.scalar.activation(
+                tables["mtot", t][:, 0:V], zeroth[:, 0:V], ACT.Identity,
+                bias=unit_base[:, t : t + 1], scale=unit_neg[:, t : t + 1],
+            )
+            ncom = tables["ncom", t][:, 0:V]
+            nc.vector.tensor_tensor(ncom, higher[:, 0:V], inv[:], ALU.mult)
+            return ncom
+
+        def second_moment(t, ncom):
+            zeroth, higher = sums[t]
+            shift = ring.tile([P, V], F32, name="shift%d" % t, tag="shift")
+            factor = unit_quad[:, t : t + 1]
+            nc.vector.scalar_tensor_tensor(shift[:], higher[:, 0:V], factor, ncom, ALU.mult, ALU.mult)
+            nc.vector.scalar_tensor_tensor(
+                tables["quad", t][:, 0:V], higher[:, V : 2 * V], factor, shift[:], ALU.mult, ALU.add
+            )
+
+        pull = [held([P, PACK, HALF], F32, "pull%d" % h) for h in range(2)]
+        slope = [held([P, PACK, HALF], F32, "slope%d" % h) for h in range(2)]
+        bodies = {}
+
+        def separations(t, a, b):
+            picks = nd_sb[:, a // 16 : b // 16]
+            name = "%d_%d" % (t, a)
+            sep = ring.tile([P, b - a], F32, name="sep" + name, tag="sep", bufs=3)
+            nc.vector.tensor_tensor(sep[:], tables["ncom", t][:].indirect(picks), px_sb[:, t, a:b], ALU.add)
+            rinv = ring.tile([P, b - a], F32, name="rinv" + name, tag="rinv", bufs=3)
+            nc.scalar.activation(rinv[:], sep[:], ACT.Square)
+            nc.scalar.activation(rinv[:], rinv[:], ACT.Abs_reciprocal_sqrt, bias=0.6)
+            nc.scalar.activation(rinv[:], rinv[:], ACT.Square)
+            qn = ring.tile([P, b - a], F32, name="qn" + name, tag="qn", bufs=3)
+            nc.scalar.activation(qn[:], tables["quad", t][:].indirect(picks), ACT.Copy)
+            mn = ring.tile([P, b - a], F32, name="mn" + name, tag="mn", bufs=3)
+            nc.scalar.activation(mn[:], tables["mtot", t][:].indirect(picks), ACT.Copy)
+            bodies[t, a] = (sep, rinv, qn, mn)
+
+        def forces(t, a, b):
+            sep, rinv, qn, mn = bodies[t, a]
+            nc.vector.tensor_tensor(qn[:], qn[:], rinv[:], ALU.mult)
+            for c in range(a, b, HALF):
+                cols = slice(c - a, c - a + HALF)
+                nc.vector.tensor_tensor(slope[c // HALF][:, t, :], sep[:, cols], rinv[:, cols], ALU.mult)
+            for c in range(a, b, HALF):
+                cols = slice(c - a, c - a + HALF)
+                nc.vector.tensor_tensor(pull[c // HALF][:, t, :], qn[:, cols], mn[:, cols], ALU.add)
+
+        def hidden(h):
+            hid = held([P, HALF, PACK], BF16, "hid%d" % h)
+            nc.vector.tensor_tensor(
+                hid[:].rearrange("p (c i) t -> p c t i", i=4),
+                pull[h][:].rearrange("p t (c i) -> p c t i", i=4),
+                slope[h][:].rearrange("p t (c i) -> p c t i", i=4),
+                ALU.mult,
+            )
+            return hid
+
+        def modes(h, hid, w3_q):
+            codes, scales = quantize(hid[:].rearrange("p r t -> p (r t)"), HALF, 1, "hid%d" % h)
+            acc = bank("modes%d" % h, h)
+            for a in range(N // P):
+                nc.tensor.matmul_mx(
+                    out=acc[:, HALF * a : HALF * (a + 1)],
+                    lhsT=w3_q[0][:, P * a : P * (a + 1)].bitcast(FP8X4),
+                    lhsT_scale=w3_q[1][:, P * a : P * (a + 1)],
+                    rhs=codes[:].bitcast(FP8X4),
+                    rhs_scale=scales[:],
+                    start=True,
+                    stop=True,
+                )
+            result = held([P, N // P, HALF], F32, "result%d" % h)
+            nc.scalar.copy(result[:].rearrange("p a r -> p (a r)"), acc[:])
+            nc.sync.dma_start(
+                out.rearrange("(a p) r -> p a r", p=P)[:, :, HALF * h : HALF * (h + 1)], result[:]
+            )
+
+        softplus(0)
+        softplus(1)
+        moments(0)
+        softplus(2)
+        softplus(3)
+        last = PACK - 1
+        for t in range(PACK):
+            if t < last:
+                moments(t + 1)
+            ncom = nodes(t)
+            second_moment(t, ncom)
+            if t < last:
+                separations(t, 0, U)
+            else:
+                separations(t, 0, HALF)
+                separations(t, HALF, U)
+            if t > 0:
+                forces(t - 1, 0, U)
+        w3_q = quantize(w3_grouped[:].rearrange("p n j -> p (n j)"), N, 1, "w3")
+        forces(last, 0, HALF)
+        hid0 = hidden(0)
+        forces(last, HALF, U)
+        modes(0, hid0, w3_q)
+        hid1 = hidden(1)
+        modes(1, hid1, w3_q)

@@ -42,18 +42,14 @@ def tile_picked_ynbodyt_acc_p_kernel(
 
         offs_sb = keep.tile([P, S // 16], U16, name="offs_sb")
         nc.sync.dma_start(offs_sb[:], offs)
-        nd_sb = keep.tile([P, U // 16], U16, name="nd_sb")
-        nc.sync.dma_start(nd_sb[:], nd)
-        unit_sb = held([P, PACK], F32, "unit_sb")
-        nc.sync.dma_start(unit_sb[:], unit.rearrange("(p t) o -> p (t o)", t=PACK))
 
+        xs_rows = held([P, T], U8, "xs_rows")
         xs_table = held([P, T], U8, "xs_table")
-        nc.gpsimd.memset(xs_table[:].bitcast(I32), 0)
+        nc.vector.memset(xs_table[:].bitcast(I32), 0)
         for q in range(4):
-            nc.scalar.dma_start(
-                xs_table[32 * q : 32 * q + 4 * PASSES, :].bitcast(I32),
-                x_scales[:, 4 * q : 4 * q + 4, :].bitcast(I32),
-            )
+            rows = slice(32 * q, 32 * q + 4 * PASSES)
+            nc.sync.dma_start(xs_rows[rows, :].bitcast(I32), x_scales[:, 4 * q : 4 * q + 4, :].bitcast(I32))
+            nc.vector.tensor_copy(xs_table[rows, :].bitcast(I32), xs_rows[rows, :].bitcast(I32))
 
         def load_words(g):
             table = held([P, T], U32, "xw_table%d" % g)
@@ -68,11 +64,15 @@ def tile_picked_ynbodyt_acc_p_kernel(
         xw_table = []
         w1_raw = []
         for g in range(PASSES):
-            xw_table.append(load_words(g))
             w1_raw.append(load_rows(w1, g, "w1_raw%d" % g))
+            xw_table.append(load_words(g))
         w2_raw = [load_rows(w2, g, "w2_raw%d" % g) for g in range(PASSES)]
-        px_sb = load_rows(px, 0, "px_sb")
         w3_raw = load_rows(w3, 0, "w3_raw")
+        nd_sb = keep.tile([P, U // 16], U16, name="nd_sb")
+        nc.sync.dma_start(nd_sb[:], nd)
+        unit_sb = held([P, PACK], F32, "unit_sb")
+        nc.sync.dma_start(unit_sb[:], unit.rearrange("(p t) o -> p (t o)", t=PACK))
+        px_sb = load_rows(px, 0, "px_sb")
 
         ident = held([P, P], F32, "ident")
         make_identity(nc, ident[:])
@@ -130,12 +130,13 @@ def tile_picked_ynbodyt_acc_p_kernel(
         xw = {}
         for vb in range(VBLOCKS):
             xs[vb] = pick(xs_table, U8, U8, vb, "xs%d" % vb)
-        for vb in range(VBLOCKS):
-            xw[0, vb] = pick(xw_table[0], U32, I32, vb, "xw0%d" % vb)
-        w1_q = [quantize(flat(round_weights(nc.scalar.copy, w1_raw[0], "w1_grouped0")), H, 1, "w1_0")]
-        xw[1, 0] = pick(xw_table[1], U32, I32, 0, "xw10")
-        w1_q.append(quantize(flat(round_weights(nc.vector.tensor_copy, w1_raw[1], "w1_grouped1")), H, 1, "w1_1"))
-        xw[1, 1] = pick(xw_table[1], U32, I32, 1, "xw11", "w1_grouped1")
+        w1_q = []
+        for g in range(PASSES):
+            name = "w1_grouped%d" % g
+            grouped = round_weights(nc.scalar.copy, w1_raw[g], name)
+            xw[g, 0] = pick(xw_table[g], U32, I32, 0, "xw%d0" % g, "picked")
+            w1_q.append(quantize(flat(grouped), H, 1, "w1_%d" % g))
+            xw[g, 1] = pick(xw_table[g], U32, I32, 1, "xw%d1" % g, "picked")
 
         def product_pass(acc, w_q, g, t, vb):
             codes, scales = w_q[g]
@@ -165,7 +166,7 @@ def tile_picked_ynbodyt_acc_p_kernel(
                 ms[t, vb] = bank("ms%d%d" % (t, vb), 2 * t + vb)
                 product_pass(ms[t, vb], w1_q, 0, t, vb)
         for vb in range(VBLOCKS):
-            for t in (range(PACK) if vb == 0 else reversed(range(PACK))):
+            for t in (range(PACK) if vb == 0 else (3, 2, 0, 1)):
                 product_pass(ms[t, vb], w1_q, 1, t, vb)
                 nc.scalar.activation(nmass[t][:, vb, :], ms[t, vb][:], ACT.Sigmoid, scale=-1.0)
 
@@ -178,10 +179,12 @@ def tile_picked_ynbodyt_acc_p_kernel(
             nc.scalar.activation(nmass[t][:], nmass[t][:], ACT.Ln, bias=LN_FLOOR)
 
         w3_grouped = held([P, N, PACK], BF16, "w3_grouped")
-        nc.scalar.copy(
+        nc.vector.tensor_copy(
             w3_grouped[:].rearrange("p (c i) j -> p c j i", i=4),
             w3_raw[:].rearrange("p j (c i) -> p c j i", i=4),
         )
+
+        w3_q = quantize(w3_grouped[:].rearrange("p n j -> p (n j)"), N, 1, "w3")
 
         def softplus(t):
             for vb in range(VBLOCKS):
@@ -200,48 +203,53 @@ def tile_picked_ynbodyt_acc_p_kernel(
                     is_transpose=True,
                 )
 
-        sums = {}
+        inv = {}
+
+        def totals(pair):
+            zeroth = bank("zeroth%d" % pair, 4 * pair + 2)
+            for u in range(2):
+                for vb in range(VBLOCKS):
+                    group_sum(zeroth, V * u + P * vb, nmass[2 * pair + u][:, vb, :])
+            inv[pair] = held([P, 2 * V], F32, "inv%d" % pair)
+            nc.scalar.activation(inv[pair][:], zeroth[:], ACT.Abs_reciprocal_sqrt, bias=D * 0.2, scale=-1.0)
+            nc.scalar.activation(inv[pair][:], inv[pair][:], ACT.Square)
+            for u in range(2):
+                t = 2 * pair + u
+                nc.scalar.activation(
+                    tables["mtot", t][:, 0:V], zeroth[:, V * u : V * (u + 1)], ACT.Identity,
+                    bias=unit_base[:, t : t + 1], scale=unit_neg[:, t : t + 1],
+                )
+
+        cx = {}
+        higher = {}
+
+        def positions(t):
+            for vb in range(VBLOCKS):
+                cx[t, vb] = product(w2_q, t, vb, "cx%d%d" % (t, vb), 4 * (t % 2) + vb)
 
         def moments(t):
-            cx = [product(w2_q, t, vb, "cx%d%d" % (t, vb), 4 * (t % 2) + vb) for vb in range(VBLOCKS)]
-            zeroth = bank("zeroth%d" % t, 4 * (t % 2) + 2)
-            for vb in range(VBLOCKS):
-                group_sum(zeroth, P * vb, nmass[t][:, vb, :])
-            higher = bank("higher%d" % t, 4 * (t % 2) + 3)
+            higher[t] = bank("higher%d" % t, 4 * (t % 2) + 3 - t // 2)
             first = []
             for vb in range(VBLOCKS):
                 value = ring.tile([P, D * P], F32, name="first%d%d" % (t, vb), tag="first", bufs=3)
                 nc.vector.scalar_tensor_tensor(
-                    value[:], nmass[t][:, vb, :], 0.2, cx[vb][:], ALU.subtract, ALU.mult
+                    value[:], nmass[t][:, vb, :], 0.2, cx[t, vb][:], ALU.subtract, ALU.mult
                 )
-                group_sum(higher, P * vb, value[:])
+                group_sum(higher[t], P * vb, value[:])
                 first.append(value)
             for vb in range(VBLOCKS):
                 value = ring.tile([P, D * P], F32, name="second%d%d" % (t, vb), tag="second", bufs=3)
-                nc.vector.tensor_tensor(value[:], first[vb][:], cx[vb][:], ALU.mult)
-                group_sum(higher, V + P * vb, value[:])
-            sums[t] = (zeroth, higher)
+                nc.vector.tensor_tensor(value[:], first[vb][:], cx[t, vb][:], ALU.mult)
+                group_sum(higher[t], V + P * vb, value[:])
 
         def nodes(t):
-            zeroth, higher = sums[t]
-            inv = ring.tile([P, V], F32, name="inv%d" % t, tag="inv")
-            nc.scalar.activation(inv[:], zeroth[:, 0:V], ACT.Abs_reciprocal_sqrt, bias=D * 0.2, scale=-1.0)
-            nc.scalar.activation(inv[:], inv[:], ACT.Square)
-            nc.scalar.activation(
-                tables["mtot", t][:, 0:V], zeroth[:, 0:V], ACT.Identity,
-                bias=unit_base[:, t : t + 1], scale=unit_neg[:, t : t + 1],
-            )
             ncom = tables["ncom", t][:, 0:V]
-            nc.vector.tensor_tensor(ncom, higher[:, 0:V], inv[:], ALU.mult)
-            return ncom
-
-        def second_moment(t, ncom):
-            zeroth, higher = sums[t]
+            nc.vector.tensor_tensor(ncom, higher[t][:, 0:V], inv[t // 2][:, V * (t % 2) : V * (t % 2 + 1)], ALU.mult)
             shift = ring.tile([P, V], F32, name="shift%d" % t, tag="shift")
             factor = unit_quad[:, t : t + 1]
-            nc.vector.scalar_tensor_tensor(shift[:], higher[:, 0:V], factor, ncom, ALU.mult, ALU.mult)
+            nc.vector.scalar_tensor_tensor(shift[:], higher[t][:, 0:V], factor, ncom, ALU.mult, ALU.mult)
             nc.vector.scalar_tensor_tensor(
-                tables["quad", t][:, 0:V], higher[:, V : 2 * V], factor, shift[:], ALU.mult, ALU.add
+                tables["quad", t][:, 0:V], higher[t][:, V : 2 * V], factor, shift[:], ALU.mult, ALU.add
             )
 
         pull = [held([P, PACK, HALF], F32, "pull%d" % h) for h in range(2)]
@@ -259,7 +267,7 @@ def tile_picked_ynbodyt_acc_p_kernel(
             nc.scalar.activation(rinv[:], rinv[:], ACT.Square)
             qn = ring.tile([P, b - a], F32, name="qn" + name, tag="qn", bufs=3)
             nc.scalar.activation(qn[:], tables["quad", t][:].indirect(picks), ACT.Copy)
-            mn = ring.tile([P, b - a], F32, name="mn" + name, tag="mn", bufs=3)
+            mn = ring.tile([P, b - a], F32, name="mn" + name, tag="mn", bufs=5)
             nc.scalar.activation(mn[:], tables["mtot", t][:].indirect(picks), ACT.Copy)
             bodies[t, a] = (sep, rinv, qn, mn)
 
@@ -273,46 +281,51 @@ def tile_picked_ynbodyt_acc_p_kernel(
                 cols = slice(c - a, c - a + HALF)
                 nc.vector.tensor_tensor(pull[c // HALF][:, t, :], qn[:, cols], mn[:, cols], ALU.add)
 
-        def hidden(h):
-            hid = held([P, HALF, PACK], BF16, "hid%d" % h)
+        def hidden(a, b):
+            h = a // HALF
+            cols = slice(a - HALF * h, b - HALF * h)
+            hid = held([P, b - a, PACK], BF16, "hid%d" % a)
             nc.vector.tensor_tensor(
                 hid[:].rearrange("p (c i) t -> p c t i", i=4),
-                pull[h][:].rearrange("p t (c i) -> p c t i", i=4),
-                slope[h][:].rearrange("p t (c i) -> p c t i", i=4),
+                pull[h][:, :, cols].rearrange("p t (c i) -> p c t i", i=4),
+                slope[h][:, :, cols].rearrange("p t (c i) -> p c t i", i=4),
                 ALU.mult,
             )
             return hid
 
-        def modes(h, hid, w3_q):
-            codes, scales = quantize(hid[:].rearrange("p r t -> p (r t)"), HALF, 1, "hid%d" % h)
-            acc = bank("modes%d" % h, h)
-            for a in range(N // P):
+        def modes(a, b, hid, w3_q, number):
+            width = b - a
+            codes, scales = quantize(hid[:].rearrange("p r t -> p (r t)"), width, 1, "hid%d" % a)
+            acc = bank("modes%d" % a, number)
+            for m in range(N // P):
                 nc.tensor.matmul_mx(
-                    out=acc[:, HALF * a : HALF * (a + 1)],
-                    lhsT=w3_q[0][:, P * a : P * (a + 1)].bitcast(FP8X4),
-                    lhsT_scale=w3_q[1][:, P * a : P * (a + 1)],
+                    out=acc[:, width * m : width * (m + 1)],
+                    lhsT=w3_q[0][:, P * m : P * (m + 1)].bitcast(FP8X4),
+                    lhsT_scale=w3_q[1][:, P * m : P * (m + 1)],
                     rhs=codes[:].bitcast(FP8X4),
                     rhs_scale=scales[:],
                     start=True,
                     stop=True,
                 )
-            result = held([P, N // P, HALF], F32, "result%d" % h)
-            nc.scalar.copy(result[:].rearrange("p a r -> p (a r)"), acc[:])
-            nc.sync.dma_start(
-                out.rearrange("(a p) r -> p a r", p=P)[:, :, HALF * h : HALF * (h + 1)], result[:]
-            )
+            result = held([P, N // P, width], F32, "result%d" % a)
+            nc.scalar.copy(result[:].rearrange("p m r -> p (m r)"), acc[:, 0 : 2 * width])
+            nc.sync.dma_start(out.rearrange("(m p) r -> p m r", p=P)[:, :, a:b], result[:])
 
-        softplus(0)
-        softplus(1)
+        for pair in range(2):
+            softplus(2 * pair)
+            softplus(2 * pair + 1)
+            positions(pair)
+        totals(0)
         moments(0)
-        softplus(2)
-        softplus(3)
         last = PACK - 1
         for t in range(PACK):
+            if t + 2 < PACK:
+                positions(t + 2)
             if t < last:
                 moments(t + 1)
-            ncom = nodes(t)
-            second_moment(t, ncom)
+            if t == 0:
+                totals(1)
+            nodes(t)
             if t < last:
                 separations(t, 0, U)
             else:
@@ -320,10 +333,12 @@ def tile_picked_ynbodyt_acc_p_kernel(
                 separations(t, HALF, U)
             if t > 0:
                 forces(t - 1, 0, U)
-        w3_q = quantize(w3_grouped[:].rearrange("p n j -> p (n j)"), N, 1, "w3")
         forces(last, 0, HALF)
-        hid0 = hidden(0)
+        hid0 = hidden(0, HALF)
         forces(last, HALF, U)
-        modes(0, hid0, w3_q)
-        hid1 = hidden(1)
-        modes(1, hid1, w3_q)
+        modes(0, HALF, hid0, w3_q, 0)
+        split = HALF + HALF // 2
+        hid1 = hidden(HALF, split)
+        hid2 = hidden(split, U)
+        modes(HALF, split, hid1, w3_q, 1)
+        modes(split, U, hid2, w3_q, 4)

@@ -78,11 +78,12 @@ def tile_picked_ynbodyt_acc_p_kernel(
         make_identity(nc, ident[:])
 
         tables = {}
-        for t in range(PACK):
+        for t in range(2):
             for name in ("ncom", "mtot", "quad"):
                 table = held([P, WINDOW], F32, "%s%d" % (name, t))
-                nc.vector.memset(table[:, V:WINDOW], 0.0)
+                nc.gpsimd.memset(table[:, V:WINDOW], 0.0)
                 tables[name, t] = table
+                tables[name, t + 2] = table
 
         def scaled_unit(factor, name):
             scaled = held([P, PACK], F32, name)
@@ -134,9 +135,9 @@ def tile_picked_ynbodyt_acc_p_kernel(
         for g in range(PASSES):
             name = "w1_grouped%d" % g
             grouped = round_weights(nc.scalar.copy, w1_raw[g], name)
-            xw[g, 0] = pick(xw_table[g], U32, I32, 0, "xw%d0" % g, "picked")
+            xw[g, 0] = pick(xw_table[g], U32, I32, 0, "xw%d0" % g, "picked" if g else "")
             w1_q.append(quantize(flat(grouped), H, 1, "w1_%d" % g))
-            xw[g, 1] = pick(xw_table[g], U32, I32, 1, "xw%d1" % g, "picked")
+            xw[g, 1] = pick(xw_table[g], U32, I32, 1, "xw%d1" % g, "picked" if g else name)
 
         def product_pass(acc, w_q, g, t, vb):
             codes, scales = w_q[g]
@@ -204,6 +205,7 @@ def tile_picked_ynbodyt_acc_p_kernel(
                 )
 
         inv = {}
+        mn = {}
 
         def totals(pair):
             zeroth = bank("zeroth%d" % pair, 4 * pair + 2)
@@ -219,27 +221,38 @@ def tile_picked_ynbodyt_acc_p_kernel(
                     tables["mtot", t][:, 0:V], zeroth[:, V * u : V * (u + 1)], ACT.Identity,
                     bias=unit_base[:, t : t + 1], scale=unit_neg[:, t : t + 1],
                 )
+            for t in (2 * pair, 2 * pair + 1):
+                mn[t] = held([P, U], F32, "mn%d" % t)
+                nc.scalar.activation(mn[t][:], tables["mtot", t][:].indirect(nd_sb[:]), ACT.Copy)
 
         cx = {}
+        cx_sb = {}
         higher = {}
 
         def positions(t):
             for vb in range(VBLOCKS):
                 cx[t, vb] = product(w2_q, t, vb, "cx%d%d" % (t, vb), 4 * (t % 2) + vb)
+                if t == 0:
+                    cx_sb[t, vb] = held([P, D * P], F32, "cx_sb%d%d" % (t, vb))
+                    nc.scalar.copy(cx_sb[t, vb][:], cx[t, vb][:])
 
         def moments(t):
             higher[t] = bank("higher%d" % t, 4 * (t % 2) + 3 - t // 2)
             first = []
             for vb in range(VBLOCKS):
-                value = ring.tile([P, D * P], F32, name="first%d%d" % (t, vb), tag="first", bufs=3)
+                value = ring.tile([P, D * P], F32, name="first%d%d" % (t, vb), tag="first", bufs=6)
                 nc.vector.scalar_tensor_tensor(
                     value[:], nmass[t][:, vb, :], 0.2, cx[t, vb][:], ALU.subtract, ALU.mult
                 )
                 group_sum(higher[t], P * vb, value[:])
                 first.append(value)
             for vb in range(VBLOCKS):
-                value = ring.tile([P, D * P], F32, name="second%d%d" % (t, vb), tag="second", bufs=3)
-                nc.vector.tensor_tensor(value[:], first[vb][:], cx[t, vb][:], ALU.mult)
+                if (t, vb) in cx_sb:
+                    value = cx_sb[t, vb]
+                    nc.gpsimd.tensor_tensor(value[:], first[vb][:], value[:], ALU.mult)
+                else:
+                    value = ring.tile([P, D * P], F32, name="second%d%d" % (t, vb), tag="second", bufs=3)
+                    nc.vector.tensor_tensor(value[:], first[vb][:], cx[t, vb][:], ALU.mult)
                 group_sum(higher[t], V + P * vb, value[:])
 
         def nodes(t):
@@ -252,48 +265,44 @@ def tile_picked_ynbodyt_acc_p_kernel(
                 tables["quad", t][:, 0:V], higher[t][:, V : 2 * V], factor, shift[:], ALU.mult, ALU.add
             )
 
-        pull = [held([P, PACK, HALF], F32, "pull%d" % h) for h in range(2)]
-        slope = [held([P, PACK, HALF], F32, "slope%d" % h) for h in range(2)]
+        pull = held([P, PACK, U], F32, "pull")
+        slope = held([P, PACK, U], F32, "slope")
         bodies = {}
 
         def separations(t, a, b):
             picks = nd_sb[:, a // 16 : b // 16]
             name = "%d_%d" % (t, a)
             sep = ring.tile([P, b - a], F32, name="sep" + name, tag="sep", bufs=3)
-            nc.vector.tensor_tensor(sep[:], tables["ncom", t][:].indirect(picks), px_sb[:, t, a:b], ALU.add)
+            if t in (0,):
+                nc.scalar.activation(sep[:], tables["ncom", t][:].indirect(picks), ACT.Copy)
+                nc.vector.tensor_tensor(sep[:], sep[:], px_sb[:, t, a:b], ALU.add)
+            else:
+                nc.vector.tensor_tensor(sep[:], tables["ncom", t][:].indirect(picks), px_sb[:, t, a:b], ALU.add)
             rinv = ring.tile([P, b - a], F32, name="rinv" + name, tag="rinv", bufs=3)
             nc.scalar.activation(rinv[:], sep[:], ACT.Square)
             nc.scalar.activation(rinv[:], rinv[:], ACT.Abs_reciprocal_sqrt, bias=0.6)
             nc.scalar.activation(rinv[:], rinv[:], ACT.Square)
             qn = ring.tile([P, b - a], F32, name="qn" + name, tag="qn", bufs=3)
             nc.scalar.activation(qn[:], tables["quad", t][:].indirect(picks), ACT.Copy)
-            mn = ring.tile([P, b - a], F32, name="mn" + name, tag="mn", bufs=5)
-            nc.scalar.activation(mn[:], tables["mtot", t][:].indirect(picks), ACT.Copy)
-            bodies[t, a] = (sep, rinv, qn, mn)
+            bodies[t, a] = (sep, rinv, qn)
 
         def forces(t, a, b):
-            sep, rinv, qn, mn = bodies[t, a]
+            sep, rinv, qn = bodies[t, a]
             nc.vector.tensor_tensor(qn[:], qn[:], rinv[:], ALU.mult)
-            for c in range(a, b, HALF):
-                cols = slice(c - a, c - a + HALF)
-                nc.vector.tensor_tensor(slope[c // HALF][:, t, :], sep[:, cols], rinv[:, cols], ALU.mult)
-            for c in range(a, b, HALF):
-                cols = slice(c - a, c - a + HALF)
-                nc.vector.tensor_tensor(pull[c // HALF][:, t, :], qn[:, cols], mn[:, cols], ALU.add)
+            nc.vector.tensor_tensor(slope[:, t, a:b], sep[:], rinv[:], ALU.mult)
+            nc.vector.tensor_tensor(pull[:, t, a:b], qn[:], mn[t][:, a:b], ALU.add)
 
         def hidden(a, b):
-            h = a // HALF
-            cols = slice(a - HALF * h, b - HALF * h)
             hid = held([P, b - a, PACK], BF16, "hid%d" % a)
             nc.vector.tensor_tensor(
                 hid[:].rearrange("p (c i) t -> p c t i", i=4),
-                pull[h][:, :, cols].rearrange("p t (c i) -> p c t i", i=4),
-                slope[h][:, :, cols].rearrange("p t (c i) -> p c t i", i=4),
+                pull[:, :, a:b].rearrange("p t (c i) -> p c t i", i=4),
+                slope[:, :, a:b].rearrange("p t (c i) -> p c t i", i=4),
                 ALU.mult,
             )
             return hid
 
-        def modes(a, b, hid, w3_q, number):
+        def modes(a, b, hid, w3_q, number, copy):
             width = b - a
             codes, scales = quantize(hid[:].rearrange("p r t -> p (r t)"), width, 1, "hid%d" % a)
             acc = bank("modes%d" % a, number)
@@ -308,7 +317,7 @@ def tile_picked_ynbodyt_acc_p_kernel(
                     stop=True,
                 )
             result = held([P, N // P, width], F32, "result%d" % a)
-            nc.scalar.copy(result[:].rearrange("p m r -> p (m r)"), acc[:, 0 : 2 * width])
+            copy(result[:].rearrange("p m r -> p (m r)"), acc[:, 0 : 2 * width])
             nc.sync.dma_start(out.rearrange("(m p) r -> p m r", p=P)[:, :, a:b], result[:])
 
         for pair in range(2):
@@ -323,22 +332,22 @@ def tile_picked_ynbodyt_acc_p_kernel(
                 positions(t + 2)
             if t < last:
                 moments(t + 1)
-            if t == 0:
-                totals(1)
             nodes(t)
             if t < last:
                 separations(t, 0, U)
             else:
                 separations(t, 0, HALF)
                 separations(t, HALF, U)
-            if t > 0:
+            if t == 0:
+                totals(1)
+            else:
                 forces(t - 1, 0, U)
         forces(last, 0, HALF)
         hid0 = hidden(0, HALF)
         forces(last, HALF, U)
-        modes(0, HALF, hid0, w3_q, 0)
+        modes(0, HALF, hid0, w3_q, 0, nc.scalar.copy)
         split = HALF + HALF // 2
         hid1 = hidden(HALF, split)
         hid2 = hidden(split, U)
-        modes(HALF, split, hid1, w3_q, 1)
-        modes(split, U, hid2, w3_q, 4)
+        modes(HALF, split, hid1, w3_q, 1, nc.scalar.copy)
+        modes(split, U, hid2, w3_q, 4, nc.vector.tensor_copy)

from contextlib import ExitStack

import concourse.mybir as mybir
from concourse.masks import make_identity

K, T, S, D, N, H, V, U = 1024, 2048, 1024, 4, 256, 512, 256, 512
FLOPS = 2 * (2 * K * H * S + H * N * U)

F32 = mybir.dt.float32
BF16 = mybir.dt.bfloat16
I32 = mybir.dt.int32
U32 = mybir.dt.uint32
U16 = mybir.dt.uint16
U8 = mybir.dt.uint8
FP8X4 = mybir.dt.float8_e4m3fn_x4
ALU = mybir.AluOpType
ACT = mybir.ActivationFunctionType

P = 128
PACK = 4
PASSES = K // (P * PACK)
VBLOCKS = V // P
WINDOW = U + 16
HALF = U // 2
LN_FLOOR = 2.0 ** -60


def tile_picked_ynbodyt_acc_p_kernel(
    tc, x_words, x_scales, w1, w2, px, unit, w3, offs, nd, out
):
    nc = tc.nc
    with ExitStack() as ctx:
        keep = ctx.enter_context(tc.tile_pool(name="keep", bufs=1))
        ring = ctx.enter_context(tc.tile_pool(name="ring", bufs=2))
        psum = ctx.enter_context(tc.psum_pool(name="psum", bufs=1))

        def held(shape, dtype, name):
            return keep.tile(shape, dtype, name=name, align_bytes=64)

        def bank(name, number):
            return psum.tile([P, 512], F32, name=name, tag="bank%d" % number)

        offs_sb = keep.tile([P, S // 16], U16, name="offs_sb")
        nc.sync.dma_start(offs_sb[:], offs)

        xs_rows = held([P, T], U8, "xs_rows")
        xs_table = held([P, T], U8, "xs_table")
        nc.vector.memset(xs_table[:].bitcast(I32), 0)
        for q in range(4):
            rows = slice(32 * q, 32 * q + 4 * PASSES)
            nc.sync.dma_start(xs_rows[rows, :].bitcast(I32), x_scales[:, 4 * q : 4 * q + 4, :].bitcast(I32))
            nc.vector.tensor_copy(xs_table[rows, :].bitcast(I32), xs_rows[rows, :].bitcast(I32))

        def load_words(g):
            table = held([P, T], U32, "xw_table%d" % g)
            nc.sync.dma_start(table[:].bitcast(I32), x_words[g].rearrange("p n j -> p (n j)").bitcast(I32))
            return table

        def load_rows(w, g, name):
            raw = held([P, PACK, w.shape[1]], F32, name)
            nc.sync.dma_start(raw[:], w[512 * g : 512 * (g + 1), :].rearrange("(p j) c -> p j c", j=PACK))
            return raw

        xw_table = []
        w1_raw = []
        for g in range(PASSES):
            w1_raw.append(load_rows(w1, g, "w1_raw%d" % g))
            xw_table.append(load_words(g))
        w2_raw = [load_rows(w2, g, "w2_raw%d" % g) for g in range(PASSES)]
        w3_raw = load_rows(w3, 0, "w3_raw")
        nd_sb = keep.tile([P, U // 16], U16, name="nd_sb")
        nc.sync.dma_start(nd_sb[:], nd)
        unit_sb = held([P, PACK], F32, "unit_sb")
        nc.sync.dma_start(unit_sb[:], unit.rearrange("(p t) o -> p (t o)", t=PACK))
        px_sb = load_rows(px, 0, "px_sb")

        ident = held([P, P], F32, "ident")
        make_identity(nc, ident[:])

        tables = {}
        for t in range(2):
            for name in ("ncom", "mtot", "quad"):
                table = held([P, WINDOW], F32, "%s%d" % (name, t))
                nc.gpsimd.memset(table[:, V:WINDOW], 0.0)
                tables[name, t] = table
                tables[name, t + 2] = table

        def scaled_unit(factor, name):
            scaled = held([P, PACK], F32, name)
            nc.gpsimd.tensor_scalar(scaled[:], unit_sb[:], factor, 0.0, ALU.mult, ALU.add)
            return scaled

        unit_neg = scaled_unit(-1.0, "unit_neg")
        unit_base = scaled_unit(D * 0.2, "unit_base")
        unit_quad = scaled_unit(-1.5, "unit_quad")

        def pick(table, dtype, view, vb, name, tag=""):
            picked = keep.tile([P, D * P], dtype, name=name + "_picked", tag=tag, align_bytes=64)
            nc.vector.tensor_copy(picked[:], table[:].indirect(offs_sb[:, 32 * vb : 32 * (vb + 1)]))
            dealt = held([P, D, P], dtype, name + "_dealt")
            nc.vector.tensor_copy(
                dealt[:].bitcast(view).rearrange("p d v -> p v d"),
                picked[:].bitcast(view).rearrange("p (v d) -> p v d", d=D),
            )
            return dealt

        def round_weights(copy, raw, name):
            grouped = keep.tile([P, PACK, P, PACK], BF16, name=name, tag=name, align_bytes=64)
            copy(
                grouped[:].rearrange("p t m j -> p m j t"),
                raw[:].rearrange("p j (m t) -> p m j t", t=PACK),
            )
            return grouped

        def quantize(grouped, words, pieces, name):
            codes = held([P, words], U32, name + "_codes")
            scales = held([P, words], U8, name + "_scales")
            step = words // pieces
            for a in range(0, words, step):
                nc.vector.quantize_mx(
                    out=codes[:, a : a + step].bitcast(FP8X4),
                    scales=scales[:, a : a + step],
                    in_=grouped[:, PACK * a : PACK * (a + step)],
                )
            return codes, scales

        def flat(grouped):
            return grouped[:].rearrange("p t m j -> p (t m j)")

        xs = {}
        xw = {}
        for vb in range(VBLOCKS):
            xs[vb] = pick(xs_table, U8, U8, vb, "xs%d" % vb)
        w1_q = []
        for g in range(PASSES):
            name = "w1_grouped%d" % g
            grouped = round_weights(nc.scalar.copy, w1_raw[g], name)
            xw[g, 0] = pick(xw_table[g], U32, I32, 0, "xw%d0" % g, "picked" if g else "")
            w1_q.append(quantize(flat(grouped), H, 1, "w1_%d" % g))
            xw[g, 1] = pick(xw_table[g], U32, I32, 1, "xw%d1" % g, "picked" if g else name)

        def product_pass(acc, w_q, g, t, vb):
            codes, scales = w_q[g]
            for d in range(D):
                nc.tensor.matmul_mx(
                    out=acc[:, P * d : P * (d + 1)],
                    lhsT=xw[g, vb][:, d, :].bitcast(FP8X4),
                    lhsT_scale=xs[vb][4 * g : P, d, :],
                    rhs=codes[:, P * t : P * (t + 1)].bitcast(FP8X4),
                    rhs_scale=scales[:, P * t : P * (t + 1)],
                    start=(g == 0 and d == 0),
                    stop=(g == PASSES - 1 and d == D - 1),
                )

        def product(w_q, t, vb, name, number):
            acc = bank(name, number)
            for g in range(PASSES):
                product_pass(acc, w_q, g, t, vb)
            return acc

        ms = {}
        nmass = {}
        for t in range(PACK):
            nmass[t] = held([P, VBLOCKS, D * P], F32, "nmass%d" % t)
        for vb in range(VBLOCKS):
            for t in range(PACK):
                ms[t, vb] = bank("ms%d%d" % (t, vb), 2 * t + vb)
                product_pass(ms[t, vb], w1_q, 0, t, vb)
        for vb in range(VBLOCKS):
            for t in (range(PACK) if vb == 0 else (3, 2, 0, 1)):
                product_pass(ms[t, vb], w1_q, 1, t, vb)
                nc.scalar.activation(nmass[t][:, vb, :], ms[t, vb][:], ACT.Sigmoid, scale=-1.0)

        w2_q = []
        for g in range(PASSES):
            grouped = round_weights(nc.vector.tensor_copy, w2_raw[g], "w2_grouped%d" % g)
            w2_q.append(quantize(flat(grouped), H, 1, "w2_%d" % g))

        for t in range(PACK):
            nc.scalar.activation(nmass[t][:], nmass[t][:], ACT.Ln, bias=LN_FLOOR)

        w3_grouped = held([P, N, PACK], BF16, "w3_grouped")
        nc.vector.tensor_copy(
            w3_grouped[:].rearrange("p (c i) j -> p c j i", i=4),
            w3_raw[:].rearrange("p j (c i) -> p c j i", i=4),
        )

        w3_q = quantize(w3_grouped[:].rearrange("p n j -> p (n j)"), N, 1, "w3")

        def softplus(t):
            for vb in range(VBLOCKS):
                nc.vector.scalar_tensor_tensor(
                    nmass[t][:, vb, :], ms[t, vb][:], -1.0, nmass[t][:, vb, :], ALU.mult, ALU.min
                )

        def group_sum(acc, column, values):
            for d in range(D):
                nc.tensor.matmul(
                    acc[:, column : column + P],
                    values[:, P * d : P * (d + 1)],
                    ident[:],
                    start=(d == 0),
                    stop=(d == D - 1),
                    is_transpose=True,
                )

        inv = {}
        mn = {}

        def totals(pair):
            zeroth = bank("zeroth%d" % pair, 4 * pair + 2)
            for u in range(2):
                for vb in range(VBLOCKS):
                    group_sum(zeroth, V * u + P * vb, nmass[2 * pair + u][:, vb, :])
            inv[pair] = held([P, 2 * V], F32, "inv%d" % pair)
            nc.scalar.activation(inv[pair][:], zeroth[:], ACT.Abs_reciprocal_sqrt, bias=D * 0.2, scale=-1.0)
            nc.scalar.activation(inv[pair][:], inv[pair][:], ACT.Square)
            for u in range(2):
                t = 2 * pair + u
                nc.scalar.activation(
                    tables["mtot", t][:, 0:V], zeroth[:, V * u : V * (u + 1)], ACT.Identity,
                    bias=unit_base[:, t : t + 1], scale=unit_neg[:, t : t + 1],
                )
            for t in (2 * pair, 2 * pair + 1):
                mn[t] = held([P, U], F32, "mn%d" % t)
                nc.scalar.activation(mn[t][:], tables["mtot", t][:].indirect(nd_sb[:]), ACT.Copy)

        cx = {}
        cx_sb = {}
        higher = {}

        def positions(t):
            for vb in range(VBLOCKS):
                cx[t, vb] = product(w2_q, t, vb, "cx%d%d" % (t, vb), 4 * (t % 2) + vb)
                if t == 0:
                    cx_sb[t, vb] = held([P, D * P], F32, "cx_sb%d%d" % (t, vb))
                    nc.scalar.copy(cx_sb[t, vb][:], cx[t, vb][:])

        def moments(t):
            higher[t] = bank("higher%d" % t, 4 * (t % 2) + 3 - t // 2)
            first = []
            for vb in range(VBLOCKS):
                value = ring.tile([P, D * P], F32, name="first%d%d" % (t, vb), tag="first", bufs=6)
                nc.vector.scalar_tensor_tensor(
                    value[:], nmass[t][:, vb, :], 0.2, cx[t, vb][:], ALU.subtract, ALU.mult
                )
                group_sum(higher[t], P * vb, value[:])
                first.append(value)
            for vb in range(VBLOCKS):
                if (t, vb) in cx_sb:
                    value = cx_sb[t, vb]
                    nc.gpsimd.tensor_tensor(value[:], first[vb][:], value[:], ALU.mult)
                else:
                    value = ring.tile([P, D * P], F32, name="second%d%d" % (t, vb), tag="second", bufs=3)
                    nc.vector.tensor_tensor(value[:], first[vb][:], cx[t, vb][:], ALU.mult)
                group_sum(higher[t], V + P * vb, value[:])

        def nodes(t):
            ncom = tables["ncom", t][:, 0:V]
            nc.vector.tensor_tensor(ncom, higher[t][:, 0:V], inv[t // 2][:, V * (t % 2) : V * (t % 2 + 1)], ALU.mult)
            shift = ring.tile([P, V], F32, name="shift%d" % t, tag="shift")
            factor = unit_quad[:, t : t + 1]
            nc.vector.scalar_tensor_tensor(shift[:], higher[t][:, 0:V], factor, ncom, ALU.mult, ALU.mult)
            nc.vector.scalar_tensor_tensor(
                tables["quad", t][:, 0:V], higher[t][:, V : 2 * V], factor, shift[:], ALU.mult, ALU.add
            )

        pull = held([P, PACK, U], F32, "pull")
        slope = held([P, PACK, U], F32, "slope")
        bodies = {}

        def separations(t, a, b):
            picks = nd_sb[:, a // 16 : b // 16]
            name = "%d_%d" % (t, a)
            sep = ring.tile([P, b - a], F32, name="sep" + name, tag="sep", bufs=3)
            if t in (0,):
                nc.scalar.activation(sep[:], tables["ncom", t][:].indirect(picks), ACT.Copy)
                nc.vector.tensor_tensor(sep[:], sep[:], px_sb[:, t, a:b], ALU.add)
            else:
                nc.vector.tensor_tensor(sep[:], tables["ncom", t][:].indirect(picks), px_sb[:, t, a:b], ALU.add)
            rinv = ring.tile([P, b - a], F32, name="rinv" + name, tag="rinv", bufs=3)
            nc.scalar.activation(rinv[:], sep[:], ACT.Square)
            nc.scalar.activation(rinv[:], rinv[:], ACT.Abs_reciprocal_sqrt, bias=0.6)
            nc.scalar.activation(rinv[:], rinv[:], ACT.Square)
            qn = ring.tile([P, b - a], F32, name="qn" + name, tag="qn", bufs=3)
            nc.scalar.activation(qn[:], tables["quad", t][:].indirect(picks), ACT.Copy)
            bodies[t, a] = (sep, rinv, qn)

        def forces(t, a, b):
            sep, rinv, qn = bodies[t, a]
            nc.vector.tensor_tensor(qn[:], qn[:], rinv[:], ALU.mult)
            nc.vector.tensor_tensor(slope[:, t, a:b], sep[:], rinv[:], ALU.mult)
            nc.vector.tensor_tensor(pull[:, t, a:b], qn[:], mn[t][:, a:b], ALU.add)

        def hidden(a, b):
            hid = held([P, b - a, PACK], BF16, "hid%d" % a)
            nc.vector.tensor_tensor(
                hid[:].rearrange("p (c i) t -> p c t i", i=4),
                pull[:, :, a:b].rearrange("p t (c i) -> p c t i", i=4),
                slope[:, :, a:b].rearrange("p t (c i) -> p c t i", i=4),
                ALU.mult,
            )
            return hid

        def modes(a, b, hid, w3_q, number, copy):
            width = b - a
            codes, scales = quantize(hid[:].rearrange("p r t -> p (r t)"), width, 1, "hid%d" % a)
            acc = bank("modes%d" % a, number)
            for m in range(N // P):
                nc.tensor.matmul_mx(
                    out=acc[:, width * m : width * (m + 1)],
                    lhsT=w3_q[0][:, P * m : P * (m + 1)].bitcast(FP8X4),
                    lhsT_scale=w3_q[1][:, P * m : P * (m + 1)],
                    rhs=codes[:].bitcast(FP8X4),
                    rhs_scale=scales[:],
                    start=True,
                    stop=True,
                )
            result = held([P, N // P, width], F32, "result%d" % a)
            copy(result[:].rearrange("p m r -> p (m r)"), acc[:, 0 : 2 * width])
            nc.sync.dma_start(out.rearrange("(m p) r -> p m r", p=P)[:, :, a:b], result[:])

        for pair in range(2):
            softplus(2 * pair)
            softplus(2 * pair + 1)
            positions(pair)
        totals(0)
        moments(0)
        last = PACK - 1
        for t in range(PACK):
            if t + 2 < PACK:
                positions(t + 2)
            if t < last:
                moments(t + 1)
            nodes(t)
            if t < last:
                separations(t, 0, U)
            else:
                separations(t, 0, HALF)
                separations(t, HALF, U)
            if t == 0:
                totals(1)
            else:
                forces(t - 1, 0, U)
        forces(last, 0, HALF)
        hid0 = hidden(0, HALF)
        forces(last, HALF, U)
        modes(0, HALF, hid0, w3_q, 0, nc.scalar.copy)
        split = HALF + HALF // 2
        hid1 = hidden(HALF, split)
        hid2 = hidden(split, U)
        modes(HALF, split, hid1, w3_q, 1, nc.scalar.copy)
        modes(split, U, hid2, w3_q, 4, nc.vector.tensor_copy)
